import numpy as np, ml_dtypes
CORES = [16,23,24,31,64,71]
N = 6
QP = 128
def setup_inputs(rng):
    m = 150 * rng.standard_normal((1, QP, 1), dtype=np.float32) + 3 * rng.standard_normal((N, QP, 1), dtype=np.float32)
    m = (m + rng.uniform(100, 300, (1, QP, 1)) * (rng.random((1, QP, 1)) < 0.7) * (rng.random((N, QP, 1)) < 0.5)).astype(np.float32)
    l = 20 * (1 + np.abs(rng.standard_normal((N, QP, 1), dtype=np.float32)))
    return {"o": (l * rng.standard_normal((N, QP, 128), dtype=np.float32) / 4).astype(ml_dtypes.bfloat16), "ml": np.concatenate([m, l], axis=2)}
def setup_inputs_big(rng):
    d = setup_inputs(rng)
    for k in ("o",): d[k] = (d[k].astype(np.float32) * 1048576.0).astype(d[k].dtype)
    return d
def setup_inputs_small(rng):
    d = setup_inputs(rng)
    for k in ("o",): d[k] = (d[k].astype(np.float32) * (1 / 1048576.0)).astype(d[k].dtype)
    return d
def setup_inputs_apart(rng):
    d = setup_inputs(rng)
    f = (10.0 ** rng.permutation(np.linspace(-1.5, 1.5, N))).astype(np.float32).reshape(N, 1, 1)
    for k in ("o",): d[k] = (d[k].astype(np.float32) * f).astype(d[k].dtype)
    return d
def reference(o, ml):
    O, ML = o.astype(np.float64), ml.astype(np.float64)
    m, l = ML[:, :, 0:1], ML[:, :, 1:2]
    f = np.exp(m - m.max(axis=0))
    y = ((f * O).sum(axis=0) / (f * l).sum(axis=0)).astype(ml_dtypes.bfloat16)
    return {"y": np.broadcast_to(y, (N,) + y.shape)}

@@ -1,0 +1,223 @@
+from concourse.bass import DstId, RemoteDMATransfer
+from concourse.mybir import AluOpType, AxisListType, ActivationFunctionType
+
+D = 128
+META = 8
+W = META + D
+C_MID, C_HI, C_L = 5, 6, 7
+PAIR = 2
+NLATE = 4
+PRE = PAIR + NLATE
+NF = NLATE + 1
+
+SCRATCH = {
+    "slots": ("sbuf", [128, (PRE + 1) * W], "bfloat16"),
+    "mlown": ("sbuf", [128, 2], "float32"),
+    "ones": ("sbuf", [128, 128], "bfloat16"),
+    "ident": ("sbuf", [128, 128], "bfloat16"),
+    "dg": ("sbuf", [128, (PAIR + NF) * 128], "bfloat16"),
+    "m2": ("sbuf", [128, PAIR], "float32"),
+    "nm1": ("sbuf", [128, 1], "float32"),
+    "f2": ("sbuf", [128, PAIR], "bfloat16"),
+    "m5": ("sbuf", [128, NF], "float32"),
+    "nm": ("sbuf", [128, 1], "float32"),
+    "f5": ("sbuf", [128, NF], "bfloat16"),
+    "fl": ("sbuf", [128, NF], "float32"),
+    "den": ("sbuf", [128, 1], "float32"),
+    "rden": ("sbuf", [128, 1], "float32"),
+    "yout": ("sbuf", [128, D], "bfloat16"),
+    "ps1": ("psum", [128, 512], "float32"),
+    "ps2": ("psum", [128, 512], "float32"),
+}
+SEMAPHORES = ["ld_o", "ld_ml", "ones", "ident", "pad", "hi", "mid", "h1", "late", "sent",
+              "m2", "mx1", "nm1", "f2", "pa", "pb", "pmm", "pre",
+              "m5", "nm", "f5", "dg0", "dg1", "dg2", "dg3", "dg4", "fl", "den", "rden", "mm", "y", "st"]
+
+
+def _plan(T, topo):
+    group = list(T.cores)
+    chips, members = [], {}
+    for c in group:
+        ch = topo.chip(c)
+        if ch not in members:
+            chips.append(ch)
+            members[ch] = []
+        members[ch].append(c)
+    carrier = {}
+    for s in chips:
+        todo = [d for d in chips if d != s]
+
+        def reach(c):
+            return [d for d in todo if all(topo.may_write(c, x) for x in members[d])]
+
+        dies = []
+        for c in sorted(members[s], key=lambda c: len(reach(c))):
+            can = sorted(reach(c), key=lambda d: topo.mates(s, d))
+            if can:
+                for j in members[s]:
+                    carrier[(j, can[0])] = c
+                todo.remove(can[0])
+                dies.append(topo.die(c))
+        spare = [c for c in range(topo.CORES_PER_CHIP * topo.CHIPS) if topo.chip(c) == s and c not in group]
+        for d in todo:
+            for j in members[s]:
+                can = [c for c in spare if all(topo.may_write(c, x) for x in members[d])]
+                can.sort(key=lambda c: dies.count(topo.die(c)))
+                carrier[(j, d)] = can[0]
+                spare.remove(can[0])
+    return chips, members, carrier
+
+
+def _masks(T, topo, c):
+    far, on = -1, -1
+    for d in T.cores:
+        if d != c:
+            if topo.chip(d) == topo.chip(c):
+                on &= topo.mask(c, d)
+            else:
+                far &= topo.mask(c, d)
+    return far, on & ~far
+
+
+def _count(mask):
+    return bin(mask).count("1")
+
+
+def rank_program(g, core, T, topo):
+    chips, members, carrier = _plan(T, topo)
+    here = topo.chip(core)
+    if here not in members:
+        return
+    pair = members[here]
+    away = [d for d in chips if d != here]
+    carried = [(j, d) for j in pair for d in away if carrier[(j, d)] == core]
+    rank = T.rank_of(core)
+    if rank is None and not carried:
+        return
+    sem, S = T.sem, T.slots
+    far, near = _masks(T, topo, core)
+    sent = [0]
+
+    def slot(k, n=1):
+        return S[:, k * W:(k + n) * W]
+
+    def write(src, targets, mask, remote_sem):
+        ids = []
+        for c, _ap in targets:
+            rid, pid, _se = topo.addr(c)
+            ids.append(DstId(rid=rid, pnc=pid))
+        g.remote_dma_fused([RemoteDMATransfer(dst_ids=ids, dma_engine_mask=mask, remote_sem=remote_sem,
+                                              srcs=[src], dsts=[ap for _c, ap in targets], alu_op=0)],
+                           local_sem=sem.sent)
+        sent[0] += _count(mask)
+
+    def carry(j):
+        k = pair.index(j)
+        targets = []
+        for jj, d in carried:
+            if jj == j:
+                land = PAIR + PAIR * [c for c in chips if c != d].index(here) + k
+                targets += [(x, slot(land)) for x in members[d]]
+        if targets:
+            write(slot(k), targets, far, sem.late)
+
+    wanted = [j for j in pair if j != core and (rank is not None or (j in [x for x, _d in carried]))]
+    n_h1 = sum(_count(_masks(T, topo, j)[1]) for j in wanted)
+
+    if rank is None:
+        g.wait_ge(sem.h1, n_h1)
+        for j in wanted:
+            carry(j)
+        g.wait_ge(sem.sent, sent[0])
+        return
+
+    n_late = sum(_count(_masks(T, topo, carrier[(j, here)])[0]) for s in away for j in members[s])
+    v, a, pe, sy = g.vector, g.scalar, g.tensor, g.sync
+    mult, add, sub, mx = AluOpType.mult, AluOpType.add, AluOpType.subtract, AluOpType.max
+    mine = pair.index(core)
+    own = mine * W
+
+    def col(c, first, n):
+        return S[:, first * W + c:(first + n - 1) * W + c + 1:W]
+
+    sy.dma_start(S[:, own + META:own + W], T.o[:, :]).then_inc(sem.ld_o, 16)
+    a.dma_start(T.mlown[:, :], T.ml[:, :]).then_inc(sem.ld_ml, 16)
+    v.memset(T.ones[:, :], 1.0).then_inc(sem.ones, 1)
+    v.memset(S[:, own:own + C_MID], 0.0).then_inc(sem.pad, 1)
+    g.wait_ge(sem.ones, 1)
+    g.affine_select(T.ident[:, :], T.ones[:, :], [[-1, 128]], AluOpType.is_equal, 0.0, 0, 1).then_inc(sem.ident, 1)
+    v.wait_ge(sem.ld_ml, 16)
+    v.tensor_copy(S[:, own + C_HI:own + C_L + 1], T.mlown[:, 0:2]).then_inc(sem.hi, 1)
+    v.wait_ge(sem.hi, 1)
+    v.tensor_tensor(S[:, own + C_MID:own + C_MID + 1], T.mlown[:, 0:1], S[:, own + C_HI:own + C_HI + 1],
+                    sub).then_inc(sem.mid, 1)
+
+    g.wait_ge(sem.ld_o, 16)
+    g.wait_ge(sem.pad, 1)
+    g.wait_ge(sem.hi, 1)
+    g.wait_ge(sem.mid, 1)
+    helpers = [carrier[(core, d)] for d in away if carrier[(core, d)] not in pair]
+    write(slot(mine), [(c, slot(mine)) for c in helpers + [j for j in pair if j != core]], near, sem.h1)
+    carry(core)
+    if [j for j, _d in carried if j != core]:
+        g.wait_ge(sem.h1, n_h1)
+        for j in pair:
+            if j != core:
+                carry(j)
+
+    v.wait_ge(sem.h1, n_h1)
+    v.wait_ge(sem.mid, 1)
+    v.tensor_tensor(T.m2[:, :], col(C_HI, 0, PAIR), col(C_MID, 0, PAIR), add).then_inc(sem.m2, 1)
+    v.wait_ge(sem.m2, 1)
+    v.tensor_reduce(T.nm1[:, :], T.m2[:, :], AxisListType.X, mx, negate=True).then_inc(sem.nm1, 1)
+    v.tensor_reduce(T.m5[:, NLATE:NF], T.m2[:, :], AxisListType.X, mx).then_inc(sem.mx1, 1)
+    a.wait_ge(sem.m2, 1)
+    a.wait_ge(sem.nm1, 1)
+    a.activation(T.f2[:, :], T.m2[:, :], ActivationFunctionType.Exp, bias=T.nm1[:, 0:1]).then_inc(sem.f2, 1)
+    v.wait_ge(sem.f2, 1)
+    v.wait_ge(sem.ident, 1)
+    v.tensor_scalar(T.dg[:, 0:128], T.ident[:, :], T.f2[:, 0:1], None, mult).then_inc(sem.pa, 1)
+    v.tensor_scalar(T.dg[:, 128:256], T.ident[:, :], T.f2[:, 1:2], None, mult).then_inc(sem.pb, 1)
+    pe.wait_ge(sem.ld_o, 16)
+    pe.wait_ge(sem.hi, 1)
+    pe.wait_ge(sem.h1, n_h1)
+    pe.wait_ge(sem.pa, 1)
+    pe.matmul(T.ps1[:, 0:D + 1], T.dg[:, 0:128], S[:, C_L:W], True, False)
+    pe.wait_ge(sem.pb, 1)
+    pe.matmul(T.ps1[:, 0:D + 1], T.dg[:, 128:256], S[:, W + C_L:2 * W], False, True).then_inc(sem.pmm, 1)
+    a.wait_ge(sem.pmm, 1)
+    a.activation(S[:, PRE * W + C_L:(PRE + 1) * W], T.ps1[:, 0:D + 1], ActivationFunctionType.Copy).then_inc(sem.pre, 1)
+
+    v.wait_ge(sem.late, n_late)
+    v.tensor_tensor(T.m5[:, 0:NLATE], col(C_HI, PAIR, NLATE), col(C_MID, PAIR, NLATE), add).then_inc(sem.m5, 1)
+    v.wait_ge(sem.m5, 1)
+    v.wait_ge(sem.mx1, 1)
+    v.tensor_reduce(T.nm[:, :], T.m5[:, :], AxisListType.X, mx, negate=True).then_inc(sem.nm, 1)
+    a.wait_ge(sem.m5, 1)
+    a.wait_ge(sem.mx1, 1)
+    a.wait_ge(sem.nm, 1)
+    a.activation(T.f5[:, :], T.m5[:, :], ActivationFunctionType.Exp, bias=T.nm[:, 0:1]).then_inc(sem.f5, 1)
+    v.wait_ge(sem.f5, 1)
+    pe.wait_ge(sem.late, n_late)
+    for k in range(NF):
+        lo = (PAIR + k) * 128
+        v.tensor_scalar(T.dg[:, lo:lo + 128], T.ident[:, :], T.f5[:, k:k + 1], None, mult).then_inc(sem["dg%d" % k], 1)
+        pe.wait_ge(sem["dg%d" % k], 1)
+        if k == NF - 1:
+            pe.wait_ge(sem.pre, 1)
+        mm = pe.matmul(T.ps2[:, 0:D], T.dg[:, lo:lo + 128], S[:, (PAIR + k) * W + META:(PAIR + k + 1) * W],
+                       k == 0, k == NF - 1)
+    mm.then_inc(sem.mm, 1)
+    v.wait_ge(sem.pre, 1)
+    v.tensor_tensor(T.fl[:, :], T.f5[:, :], col(C_L, PAIR, NF), mult).then_inc(sem.fl, 1)
+    v.wait_ge(sem.fl, 1)
+    v.tensor_reduce(T.den[:, :], T.fl[:, :], AxisListType.X, add).then_inc(sem.den, 1)
+    v.wait_ge(sem.den, 1)
+    v.reciprocal(T.rden[:, :], T.den[:, :]).then_inc(sem.rden, 1)
+    v.wait_ge(sem.rden, 1)
+    v.wait_ge(sem.mm, 1)
+    v.tensor_scalar(T.yout[:, :], T.ps2[:, 0:D], T.rden[:, 0:1], None, mult).then_inc(sem.y, 1)
+    sy.wait_ge(sem.y, 1)
+    sy.dma_start(T.y[:, :], T.yout[:, :]).then_inc(sem.st, 16)
+    sy.wait_ge(sem.st, 16)
+    g.wait_ge(sem.sent, sent[0])

@@ -12,11 +12,10 @@ NF = NLATE + 1
 
 SCRATCH = {
     "slots": ("sbuf", [128, (PRE + 1) * W], "bfloat16"),
-    "mlown": ("sbuf", [128, 2], "float32"),
+    "mlpair": ("sbuf", [128, 2 * PAIR], "float32"),
     "ones": ("sbuf", [128, 128], "bfloat16"),
     "ident": ("sbuf", [128, 128], "bfloat16"),
     "dg": ("sbuf", [128, (PAIR + NF) * 128], "bfloat16"),
-    "m2": ("sbuf", [128, PAIR], "float32"),
     "nm1": ("sbuf", [128, 1], "float32"),
     "f2": ("sbuf", [128, PAIR], "bfloat16"),
     "m5": ("sbuf", [128, NF], "float32"),
@@ -29,8 +28,8 @@ SCRATCH = {
     "ps1": ("psum", [128, 512], "float32"),
     "ps2": ("psum", [128, 512], "float32"),
 }
-SEMAPHORES = ["ld_o", "ld_ml", "ones", "ident", "pad", "hi", "mid", "h1", "late", "sent",
-              "m2", "mx1", "nm1", "f2", "pa", "pb", "pmm", "pre",
+SEMAPHORES = ["ld_o", "ld_ml", "ones", "ident", "pad", "hi", "mid", "hm", "h1", "mt", "o2", "o3", "o4", "o5", "sent",
+              "mx1", "nm1", "f2", "pa", "pb", "pmm", "pre",
               "m5", "nm", "f5", "dg0", "dg1", "dg2", "dg3", "dg4", "fl", "den", "rden", "mm", "y", "st"]
 
 
@@ -98,28 +97,35 @@ def rank_program(g, core, T, topo):
     far, near = _masks(T, topo, core)
     sent = [0]
 
-    def slot(k, n=1):
-        return S[:, k * W:(k + n) * W]
+    def part(k, lo, hi):
+        return S[:, k * W + lo:k * W + hi]
 
-    def write(src, targets, mask, remote_sem):
+    def send(src, cores, dsts, mask, remote_sem):
         ids = []
-        for c, _ap in targets:
+        for c in cores:
             rid, pid, _se = topo.addr(c)
             ids.append(DstId(rid=rid, pnc=pid))
         g.remote_dma_fused([RemoteDMATransfer(dst_ids=ids, dma_engine_mask=mask, remote_sem=remote_sem,
-                                              srcs=[src], dsts=[ap for _c, ap in targets], alu_op=0)],
-                           local_sem=sem.sent)
+                                              srcs=[src], dsts=dsts, alu_op=0)], local_sem=sem.sent)
         sent[0] += _count(mask)
+
+    def write(k, lo, hi, targets, mask, remote_sem):
+        send(part(k, lo, hi), [c for c, _land in targets], [part(land, lo, hi) for _c, land in targets], mask, remote_sem)
+
+    def landing(s, d, k):
+        return PAIR + PAIR * [c for c in chips if c != d].index(s) + k
 
     def carry(j):
         k = pair.index(j)
-        targets = []
         for jj, d in carried:
             if jj == j:
-                land = PAIR + PAIR * [c for c in chips if c != d].index(here) + k
-                targets += [(x, slot(land)) for x in members[d]]
-        if targets:
-            write(slot(k), targets, far, sem.late)
+                land = landing(here, d, k)
+                targets = [(x, land) for x in members[d]]
+                if j == core:
+                    write(k, 0, W, targets, far, sem["o%d" % land])
+                else:
+                    write(k, 0, META, targets, far, sem.mt)
+                    write(k, META, W, targets, far, sem["o%d" % land])
 
     wanted = [j for j in pair if j != core and (rank is not None or (j in [x for x, _d in carried]))]
     n_h1 = sum(_count(_masks(T, topo, j)[1]) for j in wanted)
@@ -131,49 +137,60 @@ def rank_program(g, core, T, topo):
         g.wait_ge(sem.sent, sent[0])
         return
 
-    n_late = sum(_count(_masks(T, topo, carrier[(j, here)])[0]) for s in away for j in members[s])
+    due = []
+    for s in away:
+        for k, j in enumerate(members[s]):
+            c = carrier[(j, here)]
+            due.append((0 if c == j else 1 if c in T.cores else 2, landing(s, here, k), _count(_masks(T, topo, c)[0]), c != j))
+    due.sort()
+    n_mt = sum(n for _t, _land, n, apart in due if apart)
+
     v, a, pe, sy = g.vector, g.scalar, g.tensor, g.sync
     mult, add, sub, mx = AluOpType.mult, AluOpType.add, AluOpType.subtract, AluOpType.max
     mine = pair.index(core)
     own = mine * W
+    others = [j for j in pair if j != core]
+    ML = T.mlpair
+    myml = ML[:, 2 * mine:2 * mine + 2]
+    mcols = ML[:, 0:2 * PAIR - 1:2]
 
     def col(c, first, n):
         return S[:, first * W + c:(first + n - 1) * W + c + 1:W]
 
+    a.dma_start(myml, T.ml[:, :]).then_inc(sem.ld_ml, 16)
     sy.dma_start(S[:, own + META:own + W], T.o[:, :]).then_inc(sem.ld_o, 16)
-    a.dma_start(T.mlown[:, :], T.ml[:, :]).then_inc(sem.ld_ml, 16)
     v.memset(T.ones[:, :], 1.0).then_inc(sem.ones, 1)
     v.memset(S[:, own:own + C_MID], 0.0).then_inc(sem.pad, 1)
     g.wait_ge(sem.ones, 1)
     g.affine_select(T.ident[:, :], T.ones[:, :], [[-1, 128]], AluOpType.is_equal, 0.0, 0, 1).then_inc(sem.ident, 1)
     v.wait_ge(sem.ld_ml, 16)
-    v.tensor_copy(S[:, own + C_HI:own + C_L + 1], T.mlown[:, 0:2]).then_inc(sem.hi, 1)
+    v.tensor_copy(S[:, own + C_HI:own + C_L + 1], myml).then_inc(sem.hi, 1)
     v.wait_ge(sem.hi, 1)
-    v.tensor_tensor(S[:, own + C_MID:own + C_MID + 1], T.mlown[:, 0:1], S[:, own + C_HI:own + C_HI + 1],
+    v.tensor_tensor(S[:, own + C_MID:own + C_MID + 1], ML[:, 2 * mine:2 * mine + 1], S[:, own + C_HI:own + C_HI + 1],
                     sub).then_inc(sem.mid, 1)
 
+    g.wait_ge(sem.ld_ml, 16)
+    send(myml, others, [myml for _j in others], near, sem.hm)
+    n_hm = sum(_count(_masks(T, topo, j)[1]) for j in others)
     g.wait_ge(sem.ld_o, 16)
     g.wait_ge(sem.pad, 1)
     g.wait_ge(sem.hi, 1)
     g.wait_ge(sem.mid, 1)
     helpers = [carrier[(core, d)] for d in away if carrier[(core, d)] not in pair]
-    write(slot(mine), [(c, slot(mine)) for c in helpers + [j for j in pair if j != core]], near, sem.h1)
+    write(mine, 0, W, [(c, mine) for c in helpers + others], near, sem.h1)
     carry(core)
     if [j for j, _d in carried if j != core]:
         g.wait_ge(sem.h1, n_h1)
-        for j in pair:
-            if j != core:
-                carry(j)
+        for j in others:
+            carry(j)
 
-    v.wait_ge(sem.h1, n_h1)
-    v.wait_ge(sem.mid, 1)
-    v.tensor_tensor(T.m2[:, :], col(C_HI, 0, PAIR), col(C_MID, 0, PAIR), add).then_inc(sem.m2, 1)
-    v.wait_ge(sem.m2, 1)
-    v.tensor_reduce(T.nm1[:, :], T.m2[:, :], AxisListType.X, mx, negate=True).then_inc(sem.nm1, 1)
-    v.tensor_reduce(T.m5[:, NLATE:NF], T.m2[:, :], AxisListType.X, mx).then_inc(sem.mx1, 1)
-    a.wait_ge(sem.m2, 1)
+    v.wait_ge(sem.hm, n_hm)
+    v.tensor_reduce(T.nm1[:, :], mcols, AxisListType.X, mx, negate=True).then_inc(sem.nm1, 1)
+    v.tensor_reduce(T.m5[:, NLATE:NF], mcols, AxisListType.X, mx).then_inc(sem.mx1, 1)
+    a.wait_ge(sem.ld_ml, 16)
+    a.wait_ge(sem.hm, n_hm)
     a.wait_ge(sem.nm1, 1)
-    a.activation(T.f2[:, :], T.m2[:, :], ActivationFunctionType.Exp, bias=T.nm1[:, 0:1]).then_inc(sem.f2, 1)
+    a.activation(T.f2[:, :], mcols, ActivationFunctionType.Exp, bias=T.nm1[:, 0:1]).then_inc(sem.f2, 1)
     v.wait_ge(sem.f2, 1)
     v.wait_ge(sem.ident, 1)
     v.tensor_scalar(T.dg[:, 0:128], T.ident[:, :], T.f2[:, 0:1], None, mult).then_inc(sem.pa, 1)
@@ -188,7 +205,10 @@ def rank_program(g, core, T, topo):
     a.wait_ge(sem.pmm, 1)
     a.activation(S[:, PRE * W + C_L:(PRE + 1) * W], T.ps1[:, 0:D + 1], ActivationFunctionType.Copy).then_inc(sem.pre, 1)
 
-    v.wait_ge(sem.late, n_late)
+    for _t, land, n, apart in due:
+        if not apart:
+            v.wait_ge(sem["o%d" % land], n)
+    v.wait_ge(sem.mt, n_mt)
     v.tensor_tensor(T.m5[:, 0:NLATE], col(C_HI, PAIR, NLATE), col(C_MID, PAIR, NLATE), add).then_inc(sem.m5, 1)
     v.wait_ge(sem.m5, 1)
     v.wait_ge(sem.mx1, 1)
@@ -198,15 +218,18 @@ def rank_program(g, core, T, topo):
     a.wait_ge(sem.nm, 1)
     a.activation(T.f5[:, :], T.m5[:, :], ActivationFunctionType.Exp, bias=T.nm[:, 0:1]).then_inc(sem.f5, 1)
     v.wait_ge(sem.f5, 1)
-    pe.wait_ge(sem.late, n_late)
-    for k in range(NF):
-        lo = (PAIR + k) * 128
+
+    order = [(PRE, 0)] + [(land, n) for _t, land, n, _apart in due]
+    for i, (land, n) in enumerate(order):
+        k = land - PAIR
+        lo = land * 128
         v.tensor_scalar(T.dg[:, lo:lo + 128], T.ident[:, :], T.f5[:, k:k + 1], None, mult).then_inc(sem["dg%d" % k], 1)
         pe.wait_ge(sem["dg%d" % k], 1)
-        if k == NF - 1:
+        if land == PRE:
             pe.wait_ge(sem.pre, 1)
-        mm = pe.matmul(T.ps2[:, 0:D], T.dg[:, lo:lo + 128], S[:, (PAIR + k) * W + META:(PAIR + k + 1) * W],
-                       k == 0, k == NF - 1)
+        else:
+            pe.wait_ge(sem["o%d" % land], n)
+        mm = pe.matmul(T.ps2[:, 0:D], T.dg[:, lo:lo + 128], part(land, META, W), i == 0, i == len(order) - 1)
     mm.then_inc(sem.mm, 1)
     v.wait_ge(sem.pre, 1)
     v.tensor_tensor(T.fl[:, :], T.f5[:, :], col(C_L, PAIR, NF), mult).then_inc(sem.fl, 1)

@@ -2,23 +2,24 @@ from concourse.bass import DstId, RemoteDMATransfer
 from concourse.mybir import AluOpType, AxisListType, ActivationFunctionType
 
 D = 128
-META = 8
-W = META + D
-C_MID, C_HI, C_L = 5, 6, 7
+H = D // 2
 PAIR = 2
 NLATE = 4
 PRE = PAIR + NLATE
 NF = NLATE + 1
 
 SCRATCH = {
-    "slots": ("sbuf", [128, (PRE + 1) * W], "bfloat16"),
+    "slots": ("sbuf", [128, (PRE + 1) * D], "bfloat16"),
+    "od": ("dram", [128, D], "bfloat16"),
+    "din": ("dram", [NLATE, 128, D], "bfloat16"),
     "mlpair": ("sbuf", [128, 2 * PAIR], "float32"),
+    "mlx": ("sbuf", [128, 2 * NF + 2], "float32"),
     "ones": ("sbuf", [128, 128], "bfloat16"),
     "ident": ("sbuf", [128, 128], "bfloat16"),
     "dg": ("sbuf", [128, (PAIR + NF) * 128], "bfloat16"),
     "nm1": ("sbuf", [128, 1], "float32"),
     "f2": ("sbuf", [128, PAIR], "bfloat16"),
-    "m5": ("sbuf", [128, NF], "float32"),
+    "fl2": ("sbuf", [128, PAIR], "float32"),
     "nm": ("sbuf", [128, 1], "float32"),
     "f5": ("sbuf", [128, NF], "bfloat16"),
     "fl": ("sbuf", [128, NF], "float32"),
@@ -27,10 +28,11 @@ SCRATCH = {
     "yout": ("sbuf", [128, D], "bfloat16"),
     "ps1": ("psum", [128, 512], "float32"),
     "ps2": ("psum", [128, 512], "float32"),
+    "ps3": ("psum", [128, 512], "float32"),
 }
-SEMAPHORES = ["ld_o", "ld_ml", "ones", "ident", "pad", "hi", "mid", "hm", "h1", "mt", "o2", "o3", "o4", "o5", "sent",
-              "mx1", "nm1", "f2", "pa", "pb", "pmm", "pre",
-              "m5", "nm", "f5", "dg0", "dg1", "dg2", "dg3", "dg4", "fl", "den", "rden", "mm", "y", "st"]
+SEMAPHORES = ["ld_o", "ld_od", "ld_ml", "ones", "ident", "hm", "h1", "mt", "o2", "o3", "o4", "o5", "x2", "x3", "x4", "x5", "sent",
+              "mx1", "nm1", "f2", "pa", "pb", "pmm", "pre", "fl2", "l1",
+              "nm", "f5", "dg0", "dg1", "dg2", "dg3", "dg4", "fl", "den", "rden", "mma", "mmb", "ya", "yb", "st"]
 
 
 def _plan(T, topo):
@@ -42,29 +44,52 @@ def _plan(T, topo):
             chips.append(ch)
             members[ch] = []
         members[ch].append(c)
-    carrier = {}
+    writer, mlsender = {}, {}
+
+    def ok(c, xs):
+        return all(topo.may_write(c, x) for x in xs)
+
     for s in chips:
         todo = [d for d in chips if d != s]
 
         def reach(c):
-            return [d for d in todo if all(topo.may_write(c, x) for x in members[d])]
+            return [d for d in todo if ok(c, members[d])]
 
-        dies = []
+        used, jobs = [], []
         for c in sorted(members[s], key=lambda c: len(reach(c))):
             can = sorted(reach(c), key=lambda d: topo.mates(s, d))
             if can:
-                for j in members[s]:
-                    carrier[(j, can[0])] = c
-                todo.remove(can[0])
-                dies.append(topo.die(c))
-        spare = [c for c in range(topo.CORES_PER_CHIP * topo.CHIPS) if topo.chip(c) == s and c not in group]
+                d = can[0]
+                todo.remove(d)
+                mlsender[(s, d)] = c
+                for x in members[d]:
+                    writer[(c, x)] = c
+                    used.append((topo.same_plane(s, d), topo.die(c)))
+                jobs += [(j, d) for j in members[s] if j != c]
         for d in todo:
-            for j in members[s]:
-                can = [c for c in spare if all(topo.may_write(c, x) for x in members[d])]
-                can.sort(key=lambda c: dies.count(topo.die(c)))
-                carrier[(j, d)] = can[0]
-                spare.remove(can[0])
-    return chips, members, carrier
+            mlsender[(s, d)] = [c for c in members[s] if ok(c, members[d])][0]
+            jobs += [(j, d) for j in members[s]]
+        spare = [c for c in range(topo.CORES_PER_CHIP * topo.CHIPS) if topo.chip(c) == s and c not in group]
+
+        def assign(units):
+            free, load, out = list(spare), list(used), {}
+            for j, d, xs in sorted(units, key=lambda u: len([c for c in spare if ok(c, u[2])])):
+                can = [c for c in free if ok(c, xs)]
+                if not can:
+                    return None
+                way = topo.same_plane(s, d)
+                can.sort(key=lambda c: (len([x for x in group if topo.may_write(c, x)]), load.count((way, topo.die(c)))))
+                free.remove(can[0])
+                for x in xs:
+                    out[(j, x)] = can[0]
+                    load.append((way, topo.die(can[0])))
+            return out
+
+        got = assign([(j, d, [x]) for j, d in jobs for x in members[d]])
+        if got is None:
+            got = assign([(j, d, members[d]) for j, d in jobs])
+        writer.update(got)
+    return chips, members, writer, mlsender
 
 
 def _masks(T, topo, c):
@@ -83,22 +108,23 @@ def _count(mask):
 
 
 def rank_program(g, core, T, topo):
-    chips, members, carrier = _plan(T, topo)
+    chips, members, writer, mlsender = _plan(T, topo)
     here = topo.chip(core)
     if here not in members:
         return
     pair = members[here]
     away = [d for d in chips if d != here]
-    carried = [(j, d) for j in pair for d in away if carrier[(j, d)] == core]
     rank = T.rank_of(core)
-    if rank is None and not carried:
+    out = [(j, d, [x for x in members[d] if writer[(j, x)] == core]) for j in pair for d in away]
+    out = [u for u in out if u[2]]
+    if rank is None and not out:
         return
     sem, S = T.sem, T.slots
     far, near = _masks(T, topo, core)
     sent = [0]
 
-    def part(k, lo, hi):
-        return S[:, k * W + lo:k * W + hi]
+    def part(k):
+        return S[:, k * D:(k + 1) * D]
 
     def send(src, cores, dsts, mask, remote_sem):
         ids = []
@@ -109,138 +135,137 @@ def rank_program(g, core, T, topo):
                                               srcs=[src], dsts=dsts, alu_op=0)], local_sem=sem.sent)
         sent[0] += _count(mask)
 
-    def write(k, lo, hi, targets, mask, remote_sem):
-        send(part(k, lo, hi), [c for c, _land in targets], [part(land, lo, hi) for _c, land in targets], mask, remote_sem)
+    def block(s, d):
+        return [c for c in chips if c != d].index(s)
 
     def landing(s, d, k):
-        return PAIR + PAIR * [c for c in chips if c != d].index(s) + k
-
-    def carry(j):
-        k = pair.index(j)
-        for jj, d in carried:
-            if jj == j:
-                land = landing(here, d, k)
-                targets = [(x, land) for x in members[d]]
-                if j == core:
-                    write(k, 0, W, targets, far, sem["o%d" % land])
-                else:
-                    write(k, 0, META, targets, far, sem.mt)
-                    write(k, META, W, targets, far, sem["o%d" % land])
-
-    wanted = [j for j in pair if j != core and (rank is not None or (j in [x for x, _d in carried]))]
-    n_h1 = sum(_count(_masks(T, topo, j)[1]) for j in wanted)
+        return PAIR + PAIR * block(s, d) + k
 
     if rank is None:
-        g.wait_ge(sem.h1, n_h1)
-        for j in wanted:
-            carry(j)
+        for j, d, xs in out:
+            g.wait_ge(sem.h1, _count(_masks(T, topo, j)[1]))
+            land = landing(here, d, pair.index(j))
+            send(T.od[:, :], xs, [part(land) for _x in xs], far, sem["o%d" % land])
         g.wait_ge(sem.sent, sent[0])
         return
 
     due = []
     for s in away:
         for k, j in enumerate(members[s]):
-            c = carrier[(j, here)]
-            due.append((0 if c == j else 1 if c in T.cores else 2, landing(s, here, k), _count(_masks(T, topo, c)[0]), c != j))
+            c = writer[(j, core)]
+            due.append((0 if c == j else 1, landing(s, here, k), _count(_masks(T, topo, c)[0])))
     due.sort()
-    n_mt = sum(n for _t, _land, n, apart in due if apart)
+    n_mt = sum(_count(_masks(T, topo, mlsender[(s, here)])[0]) for s in away)
 
     v, a, pe, sy = g.vector, g.scalar, g.tensor, g.sync
-    mult, add, sub, mx = AluOpType.mult, AluOpType.add, AluOpType.subtract, AluOpType.max
+    mult, add, mx = AluOpType.mult, AluOpType.add, AluOpType.max
     mine = pair.index(core)
-    own = mine * W
     others = [j for j in pair if j != core]
-    ML = T.mlpair
+    helpers = []
+    for d in away:
+        for x in members[d]:
+            if writer[(core, x)] != core and writer[(core, x)] not in helpers:
+                helpers.append(writer[(core, x)])
+    ML, MX = T.mlpair, T.mlx
     myml = ML[:, 2 * mine:2 * mine + 2]
     mcols = ML[:, 0:2 * PAIR - 1:2]
-
-    def col(c, first, n):
-        return S[:, first * W + c:(first + n - 1) * W + c + 1:W]
+    lcols = ML[:, 1:2 * PAIR:2]
+    m5 = MX[:, 0:2 * NF - 1:2]
+    l5 = MX[:, 1:2 * NF:2]
+    n_hm = sum(_count(_masks(T, topo, j)[1]) for j in others)
+    n_h1 = n_hm
 
     a.dma_start(myml, T.ml[:, :]).then_inc(sem.ld_ml, 16)
-    sy.dma_start(S[:, own + META:own + W], T.o[:, :]).then_inc(sem.ld_o, 16)
+    sy.dma_start(T.od[:, :], T.o[:, :]).then_inc(sem.ld_od, 16)
+    a.dma_start(part(mine), T.o[:, :]).then_inc(sem.ld_o, 16)
     v.memset(T.ones[:, :], 1.0).then_inc(sem.ones, 1)
-    v.memset(S[:, own:own + C_MID], 0.0).then_inc(sem.pad, 1)
-    g.wait_ge(sem.ones, 1)
-    g.affine_select(T.ident[:, :], T.ones[:, :], [[-1, 128]], AluOpType.is_equal, 0.0, 0, 1).then_inc(sem.ident, 1)
-    v.wait_ge(sem.ld_ml, 16)
-    v.tensor_copy(S[:, own + C_HI:own + C_L + 1], myml).then_inc(sem.hi, 1)
-    v.wait_ge(sem.hi, 1)
-    v.tensor_tensor(S[:, own + C_MID:own + C_MID + 1], ML[:, 2 * mine:2 * mine + 1], S[:, own + C_HI:own + C_HI + 1],
-                    sub).then_inc(sem.mid, 1)
 
     g.wait_ge(sem.ld_ml, 16)
     send(myml, others, [myml for _j in others], near, sem.hm)
-    n_hm = sum(_count(_masks(T, topo, j)[1]) for j in others)
+    g.wait_ge(sem.ld_od, 16)
+    if helpers:
+        send(T.od[:, :], helpers, [T.od[:, :] for _c in helpers], near, sem.h1)
+    for _j, d, xs in out:
+        land = landing(here, d, mine)
+        send(T.od[:, :], xs, [T.din[land - PAIR] for _x in xs], far, sem["o%d" % land])
     g.wait_ge(sem.ld_o, 16)
-    g.wait_ge(sem.pad, 1)
-    g.wait_ge(sem.hi, 1)
-    g.wait_ge(sem.mid, 1)
-    helpers = [carrier[(core, d)] for d in away if carrier[(core, d)] not in pair]
-    write(mine, 0, W, [(c, mine) for c in helpers + others], near, sem.h1)
-    carry(core)
-    if [j for j, _d in carried if j != core]:
-        g.wait_ge(sem.h1, n_h1)
-        for j in others:
-            carry(j)
+    send(part(mine), others, [part(mine) for _j in others], near, sem.h1)
+    mlto = [(x, block(here, d)) for d in away if mlsender[(here, d)] == core for x in members[d]]
+    if mlto:
+        g.wait_ge(sem.hm, n_hm)
+        send(ML[:, :], [x for x, _b in mlto], [MX[:, 2 * PAIR * b:2 * PAIR * (b + 1)] for _x, b in mlto], far, sem.mt)
+    g.wait_ge(sem.ones, 1)
+    g.affine_select(T.ident[:, :], T.ones[:, :], [[-1, 128]], AluOpType.is_equal, 0.0, 0, 1).then_inc(sem.ident, 1)
 
+    for t, land, n in due:
+        if t == 0:
+            sy.wait_ge(sem["o%d" % land], n)
+            sy.dma_start(part(land), T.din[land - PAIR]).then_inc(sem["x%d" % land], 16)
+
+    v.wait_ge(sem.ld_ml, 16)
     v.wait_ge(sem.hm, n_hm)
     v.tensor_reduce(T.nm1[:, :], mcols, AxisListType.X, mx, negate=True).then_inc(sem.nm1, 1)
-    v.tensor_reduce(T.m5[:, NLATE:NF], mcols, AxisListType.X, mx).then_inc(sem.mx1, 1)
+    v.tensor_reduce(MX[:, 2 * NLATE:2 * NLATE + 1], mcols, AxisListType.X, mx).then_inc(sem.mx1, 1)
     a.wait_ge(sem.ld_ml, 16)
     a.wait_ge(sem.hm, n_hm)
     a.wait_ge(sem.nm1, 1)
     a.activation(T.f2[:, :], mcols, ActivationFunctionType.Exp, bias=T.nm1[:, 0:1]).then_inc(sem.f2, 1)
+    v.wait_ge(sem.mt, n_mt)
+    v.wait_ge(sem.mx1, 1)
+    v.tensor_reduce(T.nm[:, :], m5, AxisListType.X, mx, negate=True).then_inc(sem.nm, 1)
+    a.wait_ge(sem.mt, n_mt)
+    a.wait_ge(sem.mx1, 1)
+    a.wait_ge(sem.nm, 1)
+    a.activation(T.f5[:, :], m5, ActivationFunctionType.Exp, bias=T.nm[:, 0:1]).then_inc(sem.f5, 1)
+
     v.wait_ge(sem.f2, 1)
     v.wait_ge(sem.ident, 1)
     v.tensor_scalar(T.dg[:, 0:128], T.ident[:, :], T.f2[:, 0:1], None, mult).then_inc(sem.pa, 1)
     v.tensor_scalar(T.dg[:, 128:256], T.ident[:, :], T.f2[:, 1:2], None, mult).then_inc(sem.pb, 1)
+    v.tensor_tensor(T.fl2[:, :], T.f2[:, :], lcols, mult).then_inc(sem.fl2, 1)
+    v.wait_ge(sem.fl2, 1)
+    v.tensor_reduce(MX[:, 2 * NLATE + 1:2 * NLATE + 2], T.fl2[:, :], AxisListType.X, add).then_inc(sem.l1, 1)
     pe.wait_ge(sem.ld_o, 16)
-    pe.wait_ge(sem.hi, 1)
     pe.wait_ge(sem.h1, n_h1)
     pe.wait_ge(sem.pa, 1)
-    pe.matmul(T.ps1[:, 0:D + 1], T.dg[:, 0:128], S[:, C_L:W], True, False)
+    pe.matmul(T.ps1[:, 0:D], T.dg[:, 0:128], part(0), True, False)
     pe.wait_ge(sem.pb, 1)
-    pe.matmul(T.ps1[:, 0:D + 1], T.dg[:, 128:256], S[:, W + C_L:2 * W], False, True).then_inc(sem.pmm, 1)
+    pe.matmul(T.ps1[:, 0:D], T.dg[:, 128:256], part(1), False, True).then_inc(sem.pmm, 1)
     a.wait_ge(sem.pmm, 1)
-    a.activation(S[:, PRE * W + C_L:(PRE + 1) * W], T.ps1[:, 0:D + 1], ActivationFunctionType.Copy).then_inc(sem.pre, 1)
+    a.activation(part(PRE), T.ps1[:, 0:D], ActivationFunctionType.Copy).then_inc(sem.pre, 1)
 
-    for _t, land, n, apart in due:
-        if not apart:
-            v.wait_ge(sem["o%d" % land], n)
-    v.wait_ge(sem.mt, n_mt)
-    v.tensor_tensor(T.m5[:, 0:NLATE], col(C_HI, PAIR, NLATE), col(C_MID, PAIR, NLATE), add).then_inc(sem.m5, 1)
-    v.wait_ge(sem.m5, 1)
-    v.wait_ge(sem.mx1, 1)
-    v.tensor_reduce(T.nm[:, :], T.m5[:, :], AxisListType.X, mx, negate=True).then_inc(sem.nm, 1)
-    a.wait_ge(sem.m5, 1)
-    a.wait_ge(sem.mx1, 1)
-    a.wait_ge(sem.nm, 1)
-    a.activation(T.f5[:, :], T.m5[:, :], ActivationFunctionType.Exp, bias=T.nm[:, 0:1]).then_inc(sem.f5, 1)
     v.wait_ge(sem.f5, 1)
-
-    order = [(PRE, 0)] + [(land, n) for _t, land, n, _apart in due]
-    for i, (land, n) in enumerate(order):
+    order = [(land, n, t) for t, land, n in due] + [(PRE, 0, 0)]
+    for i, (land, n, t) in enumerate(order):
         k = land - PAIR
         lo = land * 128
         v.tensor_scalar(T.dg[:, lo:lo + 128], T.ident[:, :], T.f5[:, k:k + 1], None, mult).then_inc(sem["dg%d" % k], 1)
         pe.wait_ge(sem["dg%d" % k], 1)
         if land == PRE:
             pe.wait_ge(sem.pre, 1)
+        elif t == 0:
+            pe.wait_ge(sem["x%d" % land], 16)
         else:
             pe.wait_ge(sem["o%d" % land], n)
-        mm = pe.matmul(T.ps2[:, 0:D], T.dg[:, lo:lo + 128], part(land, META, W), i == 0, i == len(order) - 1)
-    mm.then_inc(sem.mm, 1)
-    v.wait_ge(sem.pre, 1)
-    v.tensor_tensor(T.fl[:, :], T.f5[:, :], col(C_L, PAIR, NF), mult).then_inc(sem.fl, 1)
+        first, last = i == 0, i == len(order) - 1
+        mma = pe.matmul(T.ps2[:, 0:H], T.dg[:, lo:lo + 128], S[:, land * D:land * D + H], first, last)
+        mmb = pe.matmul(T.ps3[:, 0:H], T.dg[:, lo:lo + 128], S[:, land * D + H:(land + 1) * D], first, last)
+    mma.then_inc(sem.mma, 1)
+    mmb.then_inc(sem.mmb, 1)
+    v.wait_ge(sem.l1, 1)
+    v.tensor_tensor(T.fl[:, :], T.f5[:, :], l5, mult).then_inc(sem.fl, 1)
     v.wait_ge(sem.fl, 1)
     v.tensor_reduce(T.den[:, :], T.fl[:, :], AxisListType.X, add).then_inc(sem.den, 1)
     v.wait_ge(sem.den, 1)
     v.reciprocal(T.rden[:, :], T.den[:, :]).then_inc(sem.rden, 1)
     v.wait_ge(sem.rden, 1)
-    v.wait_ge(sem.mm, 1)
-    v.tensor_scalar(T.yout[:, :], T.ps2[:, 0:D], T.rden[:, 0:1], None, mult).then_inc(sem.y, 1)
-    sy.wait_ge(sem.y, 1)
+    v.wait_ge(sem.mma, 1)
+    v.tensor_scalar(T.yout[:, 0:H], T.ps2[:, 0:H], T.rden[:, 0:1], None, mult).then_inc(sem.ya, 1)
+    a.wait_ge(sem.rden, 1)
+    a.wait_ge(sem.mmb, 1)
+    a.activation(T.yout[:, H:D], T.ps3[:, 0:H], ActivationFunctionType.Copy, scale=T.rden[:, 0:1]).then_inc(sem.yb, 1)
+    sy.wait_ge(sem.ya, 1)
+    sy.wait_ge(sem.yb, 1)
     sy.dma_start(T.y[:, :], T.yout[:, :]).then_inc(sem.st, 16)
     sy.wait_ge(sem.st, 16)
     g.wait_ge(sem.sent, sent[0])

from concourse.bass import DstId, RemoteDMATransfer
from concourse.mybir import AluOpType, AxisListType, ActivationFunctionType

D = 128
H = D // 2
PAIR = 2
NLATE = 4
PRE = PAIR + NLATE
NF = NLATE + 1

SCRATCH = {
    "slots": ("sbuf", [128, (PRE + 1) * D], "bfloat16"),
    "od": ("dram", [128, D], "bfloat16"),
    "din": ("dram", [NLATE, 128, D], "bfloat16"),
    "mlpair": ("sbuf", [128, 2 * PAIR], "float32"),
    "mlx": ("sbuf", [128, 2 * NF + 2], "float32"),
    "ones": ("sbuf", [128, 128], "bfloat16"),
    "ident": ("sbuf", [128, 128], "bfloat16"),
    "dg": ("sbuf", [128, (PAIR + NF) * 128], "bfloat16"),
    "nm1": ("sbuf", [128, 1], "float32"),
    "f2": ("sbuf", [128, PAIR], "bfloat16"),
    "fl2": ("sbuf", [128, PAIR], "float32"),
    "nm": ("sbuf", [128, 1], "float32"),
    "f5": ("sbuf", [128, NF], "bfloat16"),
    "fl": ("sbuf", [128, NF], "float32"),
    "den": ("sbuf", [128, 1], "float32"),
    "rden": ("sbuf", [128, 1], "float32"),
    "yout": ("sbuf", [128, D], "bfloat16"),
    "ps1": ("psum", [128, 512], "float32"),
    "ps2": ("psum", [128, 512], "float32"),
    "ps3": ("psum", [128, 512], "float32"),
}
SEMAPHORES = ["ld_o", "ld_od", "ld_ml", "ones", "ident", "hm", "h1", "mt", "o2", "o3", "o4", "o5", "x2", "x3", "x4", "x5", "sent",
              "mx1", "nm1", "f2", "pa", "pb", "pmm", "pre", "fl2", "l1",
              "nm", "f5", "dg0", "dg1", "dg2", "dg3", "dg4", "fl", "den", "rden", "mma", "mmb", "ya", "yb", "st"]


def _plan(T, topo):
    group = list(T.cores)
    chips, members = [], {}
    for c in group:
        ch = topo.chip(c)
        if ch not in members:
            chips.append(ch)
            members[ch] = []
        members[ch].append(c)
    writer, mlsender = {}, {}

    def ok(c, xs):
        return all(topo.may_write(c, x) for x in xs)

    for s in chips:
        todo = [d for d in chips if d != s]

        def reach(c):
            return [d for d in todo if ok(c, members[d])]

        used, jobs = [], []
        for c in sorted(members[s], key=lambda c: len(reach(c))):
            can = sorted(reach(c), key=lambda d: topo.mates(s, d))
            if can:
                d = can[0]
                todo.remove(d)
                mlsender[(s, d)] = c
                for x in members[d]:
                    writer[(c, x)] = c
                    used.append((topo.same_plane(s, d), topo.die(c)))
                jobs += [(j, d) for j in members[s] if j != c]
        for d in todo:
            mlsender[(s, d)] = [c for c in members[s] if ok(c, members[d])][0]
            jobs += [(j, d) for j in members[s]]
        spare = [c for c in range(topo.CORES_PER_CHIP * topo.CHIPS) if topo.chip(c) == s and c not in group]

        def assign(units):
            free, load, out = list(spare), list(used), {}
            for j, d, xs in sorted(units, key=lambda u: len([c for c in spare if ok(c, u[2])])):
                can = [c for c in free if ok(c, xs)]
                if not can:
                    return None
                way = topo.same_plane(s, d)
                can.sort(key=lambda c: (len([x for x in group if topo.may_write(c, x)]), load.count((way, topo.die(c)))))
                free.remove(can[0])
                for x in xs:
                    out[(j, x)] = can[0]
                    load.append((way, topo.die(can[0])))
            return out

        got = assign([(j, d, [x]) for j, d in jobs for x in members[d]])
        if got is None:
            got = assign([(j, d, members[d]) for j, d in jobs])
        writer.update(got)
    return chips, members, writer, mlsender


def _masks(T, topo, c):
    far, on = -1, -1
    for d in T.cores:
        if d != c:
            if topo.chip(d) == topo.chip(c):
                on &= topo.mask(c, d)
            else:
                far &= topo.mask(c, d)
    return far, on & ~far


def _count(mask):
    return bin(mask).count("1")


def rank_program(g, core, T, topo):
    chips, members, writer, mlsender = _plan(T, topo)
    here = topo.chip(core)
    if here not in members:
        return
    pair = members[here]
    away = [d for d in chips if d != here]
    rank = T.rank_of(core)
    out = [(j, d, [x for x in members[d] if writer[(j, x)] == core]) for j in pair for d in away]
    out = [u for u in out if u[2]]
    if rank is None and not out:
        return
    sem, S = T.sem, T.slots
    far, near = _masks(T, topo, core)
    sent = [0]

    def part(k):
        return S[:, k * D:(k + 1) * D]

    def send(src, cores, dsts, mask, remote_sem):
        ids = []
        for c in cores:
            rid, pid, _se = topo.addr(c)
            ids.append(DstId(rid=rid, pnc=pid))
        g.remote_dma_fused([RemoteDMATransfer(dst_ids=ids, dma_engine_mask=mask, remote_sem=remote_sem,
                                              srcs=[src], dsts=dsts, alu_op=0)], local_sem=sem.sent)
        sent[0] += _count(mask)

    def block(s, d):
        return [c for c in chips if c != d].index(s)

    def landing(s, d, k):
        return PAIR + PAIR * block(s, d) + k

    if rank is None:
        for j, d, xs in out:
            g.wait_ge(sem.h1, _count(_masks(T, topo, j)[1]))
            land = landing(here, d, pair.index(j))
            send(T.od[:, :], xs, [part(land) for _x in xs], far, sem["o%d" % land])
        g.wait_ge(sem.sent, sent[0])
        return

    due = []
    for s in away:
        for k, j in enumerate(members[s]):
            c = writer[(j, core)]
            due.append((0 if c == j else 1, landing(s, here, k), _count(_masks(T, topo, c)[0])))
    due.sort()
    n_mt = sum(_count(_masks(T, topo, mlsender[(s, here)])[0]) for s in away)

    v, a, pe, sy = g.vector, g.scalar, g.tensor, g.sync
    mult, add, mx = AluOpType.mult, AluOpType.add, AluOpType.max
    mine = pair.index(core)
    others = [j for j in pair if j != core]
    helpers = []
    for d in away:
        for x in members[d]:
            if writer[(core, x)] != core and writer[(core, x)] not in helpers:
                helpers.append(writer[(core, x)])
    ML, MX = T.mlpair, T.mlx
    myml = ML[:, 2 * mine:2 * mine + 2]
    mcols = ML[:, 0:2 * PAIR - 1:2]
    lcols = ML[:, 1:2 * PAIR:2]
    m5 = MX[:, 0:2 * NF - 1:2]
    l5 = MX[:, 1:2 * NF:2]
    n_hm = sum(_count(_masks(T, topo, j)[1]) for j in others)
    n_h1 = n_hm

    a.dma_start(myml, T.ml[:, :]).then_inc(sem.ld_ml, 16)
    sy.dma_start(T.od[:, :], T.o[:, :]).then_inc(sem.ld_od, 16)
    a.dma_start(part(mine), T.o[:, :]).then_inc(sem.ld_o, 16)
    v.memset(T.ones[:, :], 1.0).then_inc(sem.ones, 1)

    g.wait_ge(sem.ld_ml, 16)
    send(myml, others, [myml for _j in others], near, sem.hm)
    g.wait_ge(sem.ld_od, 16)
    if helpers:
        send(T.od[:, :], helpers, [T.od[:, :] for _c in helpers], near, sem.h1)
    for _j, d, xs in out:
        land = landing(here, d, mine)
        send(T.od[:, :], xs, [T.din[land - PAIR] for _x in xs], far, sem["o%d" % land])
    g.wait_ge(sem.ld_o, 16)
    send(part(mine), others, [part(mine) for _j in others], near, sem.h1)
    mlto = [(x, block(here, d)) for d in away if mlsender[(here, d)] == core for x in members[d]]
    if mlto:
        g.wait_ge(sem.hm, n_hm)
        send(ML[:, :], [x for x, _b in mlto], [MX[:, 2 * PAIR * b:2 * PAIR * (b + 1)] for _x, b in mlto], far, sem.mt)
    g.wait_ge(sem.ones, 1)
    g.affine_select(T.ident[:, :], T.ones[:, :], [[-1, 128]], AluOpType.is_equal, 0.0, 0, 1).then_inc(sem.ident, 1)

    for t, land, n in due:
        if t == 0:
            sy.wait_ge(sem["o%d" % land], n)
            sy.dma_start(part(land), T.din[land - PAIR]).then_inc(sem["x%d" % land], 16)

    v.wait_ge(sem.ld_ml, 16)
    v.wait_ge(sem.hm, n_hm)
    v.tensor_reduce(T.nm1[:, :], mcols, AxisListType.X, mx, negate=True).then_inc(sem.nm1, 1)
    v.tensor_reduce(MX[:, 2 * NLATE:2 * NLATE + 1], mcols, AxisListType.X, mx).then_inc(sem.mx1, 1)
    a.wait_ge(sem.ld_ml, 16)
    a.wait_ge(sem.hm, n_hm)
    a.wait_ge(sem.nm1, 1)
    a.activation(T.f2[:, :], mcols, ActivationFunctionType.Exp, bias=T.nm1[:, 0:1]).then_inc(sem.f2, 1)
    v.wait_ge(sem.mt, n_mt)
    v.wait_ge(sem.mx1, 1)
    v.tensor_reduce(T.nm[:, :], m5, AxisListType.X, mx, negate=True).then_inc(sem.nm, 1)
    a.wait_ge(sem.mt, n_mt)
    a.wait_ge(sem.mx1, 1)
    a.wait_ge(sem.nm, 1)
    a.activation(T.f5[:, :], m5, ActivationFunctionType.Exp, bias=T.nm[:, 0:1]).then_inc(sem.f5, 1)

    v.wait_ge(sem.f2, 1)
    v.wait_ge(sem.ident, 1)
    v.tensor_scalar(T.dg[:, 0:128], T.ident[:, :], T.f2[:, 0:1], None, mult).then_inc(sem.pa, 1)
    v.tensor_scalar(T.dg[:, 128:256], T.ident[:, :], T.f2[:, 1:2], None, mult).then_inc(sem.pb, 1)
    v.tensor_tensor(T.fl2[:, :], T.f2[:, :], lcols, mult).then_inc(sem.fl2, 1)
    v.wait_ge(sem.fl2, 1)
    v.tensor_reduce(MX[:, 2 * NLATE + 1:2 * NLATE + 2], T.fl2[:, :], AxisListType.X, add).then_inc(sem.l1, 1)
    pe.wait_ge(sem.ld_o, 16)
    pe.wait_ge(sem.h1, n_h1)
    pe.wait_ge(sem.pa, 1)
    pe.matmul(T.ps1[:, 0:D], T.dg[:, 0:128], part(0), True, False)
    pe.wait_ge(sem.pb, 1)
    pe.matmul(T.ps1[:, 0:D], T.dg[:, 128:256], part(1), False, True).then_inc(sem.pmm, 1)
    a.wait_ge(sem.pmm, 1)
    a.activation(part(PRE), T.ps1[:, 0:D], ActivationFunctionType.Copy).then_inc(sem.pre, 1)

    v.wait_ge(sem.f5, 1)
    order = [(land, n, t) for t, land, n in due] + [(PRE, 0, 0)]
    for i, (land, n, t) in enumerate(order):
        k = land - PAIR
        lo = land * 128
        v.tensor_scalar(T.dg[:, lo:lo + 128], T.ident[:, :], T.f5[:, k:k + 1], None, mult).then_inc(sem["dg%d" % k], 1)
        pe.wait_ge(sem["dg%d" % k], 1)
        if land == PRE:
            pe.wait_ge(sem.pre, 1)
        elif t == 0:
            pe.wait_ge(sem["x%d" % land], 16)
        else:
            pe.wait_ge(sem["o%d" % land], n)
        first, last = i == 0, i == len(order) - 1
        mma = pe.matmul(T.ps2[:, 0:H], T.dg[:, lo:lo + 128], S[:, land * D:land * D + H], first, last)
        mmb = pe.matmul(T.ps3[:, 0:H], T.dg[:, lo:lo + 128], S[:, land * D + H:(land + 1) * D], first, last)
    mma.then_inc(sem.mma, 1)
    mmb.then_inc(sem.mmb, 1)
    v.wait_ge(sem.l1, 1)
    v.tensor_tensor(T.fl[:, :], T.f5[:, :], l5, mult).then_inc(sem.fl, 1)
    v.wait_ge(sem.fl, 1)
    v.tensor_reduce(T.den[:, :], T.fl[:, :], AxisListType.X, add).then_inc(sem.den, 1)
    v.wait_ge(sem.den, 1)
    v.reciprocal(T.rden[:, :], T.den[:, :]).then_inc(sem.rden, 1)
    v.wait_ge(sem.rden, 1)
    v.wait_ge(sem.mma, 1)
    v.tensor_scalar(T.yout[:, 0:H], T.ps2[:, 0:H], T.rden[:, 0:1], None, mult).then_inc(sem.ya, 1)
    a.wait_ge(sem.rden, 1)
    a.wait_ge(sem.mmb, 1)
    a.activation(T.yout[:, H:D], T.ps3[:, 0:H], ActivationFunctionType.Copy, scale=T.rden[:, 0:1]).then_inc(sem.yb, 1)
    sy.wait_ge(sem.ya, 1)
    sy.wait_ge(sem.yb, 1)
    sy.dma_start(T.y[:, :], T.yout[:, :]).then_inc(sem.st, 16)
    sy.wait_ge(sem.st, 16)
    g.wait_ge(sem.sent, sent[0])
